import numpy as np
import ml_dtypes


def mxq(x, axis, fmt="e4m3"):
    dtype, down = {"e4m3": (ml_dtypes.float8_e4m3fn, 7), "e5m2": (ml_dtypes.float8_e5m2, 14)}[fmt]
    v = np.moveaxis(np.asarray(x, np.float32).astype(ml_dtypes.bfloat16).astype(np.float64), axis, -1)
    blocks = v.reshape(v.shape[:-1] + (-1, 32))
    amax = np.abs(blocks).max(-1, keepdims=True)
    byte = np.maximum(np.where(amax > 0, np.frexp(amax)[1] - 1 + 127, 0) - down, 1)
    scale = np.exp2(byte - 127.0)
    codes = (blocks / scale).astype(np.float32).astype(dtype).astype(np.float64)
    return np.moveaxis((codes * scale).reshape(v.shape), -1, axis)


WIDE = False


def mx_kscale(k):
    if not WIDE:
        return np.ones(k)
    levels = np.array([10, -10, 5, -5, 0])
    if k % 512:
        return np.exp2(np.random.permutation(np.resize(levels, k // 32))).repeat(32)
    a = np.empty((k // 512, 16))
    for p in range(k // 512):
        a[p, :8] = np.random.permutation(np.resize(levels, 8))
        for g in range(8):
            far = levels[np.abs(levels - a[p, g]) >= 10]
            a[p, g + 8] = far[np.random.randint(len(far))]
    return np.exp2(a.ravel()).repeat(32)


BF16 = ml_dtypes.bfloat16


def bf(x):
    return np.asarray(x, np.float32).astype(BF16)


def f64(x):
    return np.asarray(x).astype(np.float64)


B, N = 1536, 1024

STEP = 0.33
HEAT = 0.3


def setup_inputs():
    s = mx_kscale(N)
    q = np.random.standard_normal((B, N)) * s
    w = STEP * np.random.standard_normal((N, N)) / np.sqrt(N) / s[:, None] * s
    heater = HEAT * np.random.standard_normal(N) * s
    inv_cap = (1 + 0.1 * np.random.standard_normal(N)) / s
    return {"q": bf(q), "w": bf(w), "heater": bf(heater), "inv_cap": bf(inv_cap)}


def reference(q, w, heater, inv_cap):
    q0, h = f64(q), f64(heater)
    wq = mxq(f64(w), 0, "e4m3")
    d1 = mxq(q0, 1, "e4m3") @ wq
    q1 = q0 + d1 + h
    d2 = mxq(q1, 1, "e4m3") @ wq
    q2 = q1 + d2 + h
    d3 = mxq(q2, 1, "e4m3") @ wq
    q3 = q2 + d3
    return q3 * f64(inv_cap)

@@ -1,0 +1,256 @@
+from contextlib import ExitStack
+
+import concourse.mybir as mybir
+from concourse.masks import make_identity
+
+B, N = 1536, 1024
+FLOPS = 3 * 2 * B * N * N
+
+F32 = mybir.dt.float32
+BF16 = mybir.dt.bfloat16
+U32 = mybir.dt.uint32
+U8 = mybir.dt.uint8
+FP8X4 = mybir.dt.float8_e4m3fn_x4
+ADD = mybir.AluOpType.add
+MULT = mybir.AluOpType.mult
+
+P = 128
+CH = 512
+NCH = B // CH
+NB = CH // P
+LOADS = ['q0b','q0a','w01','w00','q1a','w10','w11','q1b','q2a','q2b']
+WENG = {"10":"SS","11":"VS","00":"VS","01":"VS"}
+TAILV = 2
+ORDER = [
+    "turn 0 1",
+    "qq 0 1",
+    "w 01 0",
+    "turn 0 0",
+    "qq 0 0",
+    "w 00 0",
+    "w 01 1",
+    "w 00 1",
+    "wq 01",
+    "w 10 1",
+    "w 10 0",
+    "wq 00",
+    "w 11 1",
+    "turn 1 0",
+    "w 11 0",
+    "M1A003",
+    "wq 10",
+    "wq 11",
+    "turn 1 1",
+    "M1A034",
+    "il 1 0 0",
+    "qq 1 0",
+    "M1A101",
+    "qq 1 1",
+    "M1A114",
+    "turn 2 1",
+    "il 1 0 1",
+    "rq 1 0 0",
+    "M1B104",
+    "qq 2 1",
+    "il 1 1 1",
+    "M1B001",
+    "rq 1 0 1",
+    "M1B012",
+    "turn 2 0",
+    "M1B024",
+    "il 1 1 0",
+    "M2A004",
+    "il 2 0 0",
+    "qq 2 0",
+    "M2A104",
+    "il 2 0 1",
+    "M1C002",
+    "rq 2 0 0",
+    "M1C024",
+    "rq 2 0 1",
+    "il 1 2 0",
+    "M1C101",
+    "rq 1 1 1",
+    "M1C114",
+    "il 1 2 1",
+    "M3A102",
+    "rq 1 1 0",
+    "M3A124",
+    "M3A004",
+    "M2B102",
+    "rq 1 2 1",
+    "out 0 1",
+    "M2B124",
+    "out 0 0",
+    "il 2 1 1",
+    "rq 1 2 0",
+    "M2B004",
+    "il 2 1 0",
+    "M2C002",
+    "rq 2 1 1",
+    "M2C024",
+    "il 2 2 0",
+    "rq 2 1 0",
+    "M2C104",
+    "il 2 2 1",
+    "M3B104",
+    "rq 2 2 0",
+    "rq 2 2 1",
+    "M3B004",
+    "out 1 1",
+    "M3C004",
+    "M3C101",
+    "out 1 0",
+    "M3C114",
+    "out 2 0",
+    "out 2 1",
+]
+
+
+def tile_dense_heat_steps_t1_kernel(tc, q, w, heater, inv_cap, out):
+    nc = tc.nc
+    with ExitStack() as ctx:
+        keep = ctx.enter_context(tc.tile_pool(name="keep", bufs=1))
+        stage = ctx.enter_context(tc.tile_pool(name="stage", bufs=3))
+        psum = ctx.enter_context(tc.psum_pool(name="psum", bufs=8))
+        ctx.enter_context(tc.manual_schedule())
+
+        ident = keep.tile([P, P], F32, name="ident")
+        warm = keep.tile([P, 1], F32, name="warm")
+        hv = keep.tile([P, 2, 4], BF16, name="hv")
+        iv = keep.tile([P, 2, 4], BF16, name="iv")
+        wraw = [keep.tile([P, 2, 4, 512], BF16, name="wraw%d" % h) for h in range(2)]
+        wcodes = keep.tile([P, 2, N], U32, name="wcodes", align_bytes=256)
+        wscales = keep.tile([P, 2, N], U8, name="wscales", align_bytes=256)
+        qn = [keep.tile([P, NB, N], BF16, name="qn%d" % c) for c in range(NCH)]
+        qint = [keep.tile([P, 2, CH, 4], BF16, name="qint%d" % c, align_bytes=256) for c in range(NCH)]
+        state = [[keep.tile([P, 4, CH], F32, name="state%d%d" % (c, g)) for g in range(2)] for c in range(NCH)]
+
+        def hbm_rows(x, c):
+            return x[CH * c : CH * (c + 1), :].rearrange("(p b) k -> p b k", b=NB)
+
+        nc.gpsimd.dma_start(out=hv[:], in_=heater.rearrange("(g p t) -> p g t", g=2, t=4))
+        nc.gpsimd.dma_start(out=iv[:], in_=inv_cap.rearrange("(g p t) -> p g t", g=2, t=4))
+        for x in LOADS:
+            if x.startswith("w"):
+                h, g = int(x[1]), int(x[2])
+                src = w[512 * g : 512 * (g + 1), 512 * h : 512 * (h + 1)].rearrange("(p j) c -> p j c", j=4)
+                nc.sync.dma_start(out=wraw[h][:, g, :, :], in_=src)
+            else:
+                c, pr = int(x[1]), "ab".index(x[2])
+                nc.sync.dma_start(out=qn[c][:, 2 * pr : 2 * pr + 2, :], in_=hbm_rows(q, c)[:, 2 * pr : 2 * pr + 2, :])
+        nc.vector.memset(warm[:], 0.0)
+        nc.scalar.copy(out=warm[:], in_=warm[:])
+        make_identity(nc, ident[:])
+
+        codes = {}
+        wgrp = {}
+        grp = {}
+
+        def get_codes(s, c):
+            if (s, c) not in codes:
+                cd = keep.tile([P, 2, CH], U32, name="codes%d%d" % (s % 2, c), align_bytes=256)
+                sc = keep.tile([P, 2, CH], U8, name="scales%d%d" % (s % 2, c), align_bytes=256)
+                codes[(s, c)] = (cd, sc)
+            return codes[(s, c)]
+
+        def do_wq(h, g):
+            cols = slice(512 * h, 512 * (h + 1))
+            nc.vector.quantize_mx(out=wcodes[:, g, cols].bitcast(FP8X4), scales=wscales[:, g, cols], in_=wgrp[(h, g)][:])
+
+        def do_w(h, g, hf):
+            if (h, g) not in wgrp:
+                new = stage.tile([P, 2048], BF16, name="wgrp", align_bytes=256, bufs=4)
+                wgrp[(h, g)] = new
+            copy = nc.vector.tensor_copy if WENG["%d%d" % (h, g)][hf] == "V" else nc.scalar.copy
+            ts = slice(2 * hf, 2 * hf + 2)
+            copy(
+                out=wgrp[(h, g)][:].rearrange("p (t m j) -> p t m j", t=4, j=4)[:, ts],
+                in_=wraw[h][:, g, :, :].rearrange("p j (m t) -> p t m j", t=4)[:, ts],
+            )
+
+        def do_turn(c, pr):
+            for b in (2 * pr, 2 * pr + 1):
+                words = qn[c][:, b, :].bitcast(F32)
+                bank = psum.tile([P, 4, P], F32, name="bank")
+                for g in range(2):
+                    for u in range(2):
+                        nc.tensor.transpose(bank[:, 2 * g + u, :], words[:, 256 * g + u : 256 * (g + 1) : 2], ident[:])
+                dst = qint[c][:, :, P * b : P * (b + 1), :].rearrange("p g n t -> p g (n t)").bitcast(F32)
+                nc.scalar.copy(out=dst.rearrange("p g (n u) -> p g n u", u=2), in_=bank[:].rearrange("p (g u) n -> p g n u", g=2))
+
+        def do_qq(c, pr):
+            cd, sc = get_codes(1, c)
+            cols = slice(256 * pr, 256 * (pr + 1))
+            for g in range(2):
+                nc.vector.quantize_mx(out=cd[:, g, cols].bitcast(FP8X4), scales=sc[:, g, cols], in_=qint[c][:, g, cols, :].rearrange("p n t -> p (n t)"))
+
+        def do_mx(s, c, go, t):
+            cd, sc = get_codes(s, c)
+            bank = psum.tile([P, CH], F32, name="bank")
+            cols = slice(512 * go + 128 * t, 512 * go + 128 * (t + 1))
+            for g in range(2):
+                nc.tensor.matmul_mx(
+                    out=bank[:],
+                    lhsT=wcodes[:, g, cols].bitcast(FP8X4),
+                    lhsT_scale=wscales[:, g, cols],
+                    rhs=cd[:, g, :].bitcast(FP8X4),
+                    rhs_scale=sc[:, g, :],
+                    start=(g == 0),
+                    stop=(g == 1),
+                )
+            st = state[c][go][:, t, :]
+            if s == 1:
+                nc.vector.scalar_tensor_tensor(st, bank[:], hv[:, go, t : t + 1], qint[c][:, go, :, t], ADD, ADD)
+            elif s == 2:
+                nc.vector.scalar_tensor_tensor(st, bank[:], hv[:, go, t : t + 1], st, ADD, ADD)
+            else:
+                nc.vector.scalar_tensor_tensor(st, bank[:], iv[:, go, t : t + 1], st, MULT, ADD)
+
+        def do_il(s, c, go):
+            grouped = stage.tile([P, CH, 4], BF16, name="grp", align_bytes=256)
+            for n0 in (0, 256):
+                n = slice(n0, n0 + 256)
+                nc.scalar.copy(
+                    out=grouped[:, n, :].rearrange("p (c i) t -> p c t i", i=4),
+                    in_=state[c][go][:, :, n].rearrange("p t (c i) -> p c t i", i=4),
+                )
+            grp[(s, c, go)] = grouped
+            if s == 2:
+                for t in range(4):
+                    st = state[c][go][:, t, :]
+                    nc.gpsimd.tensor_scalar(st, st, iv[:, go, t : t + 1], 0.0, MULT, ADD)
+
+        def do_rq(s, c, go):
+            cd, sc = get_codes(s + 1, c)
+            nc.vector.quantize_mx(out=cd[:, go, :].bitcast(FP8X4), scales=sc[:, go, :], in_=grp[(s, c, go)][:].rearrange("p n t -> p (n t)"))
+
+        count = {"out": 0}
+
+        def do_out(c, go):
+            count["out"] += 1
+            dst = hbm_rows(out, c)
+            res = stage.tile([P, NB, 512], F32, name="res")
+            for b in range(NB):
+                bank = psum.tile([P, 4, P], F32, name="bank")
+                for t in range(4):
+                    nc.tensor.transpose(bank[:, t, :], state[c][go][:, t, P * b : P * (b + 1)], ident[:])
+                copy = nc.vector.tensor_copy if count["out"] > 6 - TAILV and b % 2 == 1 else nc.scalar.copy
+                copy(out=res[:, b, :].rearrange("p (m t) -> p m t", t=4), in_=bank[:].rearrange("p t m -> p m t"))
+                nc.sync.dma_start(out=dst[:, b, 512 * go : 512 * (go + 1)], in_=res[:, b, :])
+
+        table = {"turn": do_turn, "qq": do_qq, "il": do_il, "rq": do_rq, "out": do_out}
+        for line in ORDER:
+            if line.startswith("M"):
+                s, c, go = int(line[1]), "ABC".index(line[2]), int(line[3])
+                first = int(line[4])
+                for t in range(first, int(line[5])):
+                    do_mx(s, c, go, t)
+            else:
+                parts = line.split(" ")
+                if parts[0] == "w":
+                    do_w(int(parts[1][0]), int(parts[1][1]), int(parts[2]))
+                elif parts[0] == "wq":
+                    do_wq(int(parts[1][0]), int(parts[1][1]))
+                else:
+                    table[parts[0]](*[int(v) for v in parts[1:]])

@@ -18,92 +18,93 @@ P = 128
 CH = 512
 NCH = B // CH
 NB = CH // P
-LOADS = ['q0b','q0a','w01','w00','q1a','w10','w11','q1b','q2a','q2b']
+LOADS = ['q0a','w00','q0b','w01','q1a','w10','w11','q1b','q2b','q2a']
 WENG = {"10":"SS","11":"VS","00":"VS","01":"VS"}
 TAILV = 2
 ORDER = [
-    "turn 0 1",
-    "qq 0 1",
-    "w 01 0",
     "turn 0 0",
+    "w 00 1",
+    "turn 0 1",
     "qq 0 0",
     "w 00 0",
-    "w 01 1",
-    "w 00 1",
-    "wq 01",
-    "w 10 1",
-    "w 10 0",
     "wq 00",
-    "w 11 1",
+    "w 01 1",
     "turn 1 0",
-    "w 11 0",
-    "M1A003",
-    "wq 10",
-    "wq 11",
-    "turn 1 1",
-    "M1A034",
-    "il 1 0 0",
+    "w 01 0",
+    "qq 0 1",
+    "w 10 1",
+    "w 11 1",
+    "wq 01",
     "qq 1 0",
-    "M1A101",
+    "M1A002",
+    "w 10 0",
+    "w 11 0",
+    "M1A023",
+    "wq 11",
+    "wq 10",
+    "M1A034",
+    "turn 1 1",
+    "il 1 0 0",
     "qq 1 1",
-    "M1A114",
     "turn 2 1",
+    "M1A104",
     "il 1 0 1",
+    "M1B003",
     "rq 1 0 0",
-    "M1B104",
-    "qq 2 1",
-    "il 1 1 1",
-    "M1B001",
-    "rq 1 0 1",
-    "M1B012",
     "turn 2 0",
-    "M1B024",
+    "qq 2 1",
+    "M1B034",
     "il 1 1 0",
+    "M1B101",
+    "rq 1 0 1",
+    "M1B114",
+    "il 1 1 1",
+    "qq 2 0",
     "M2A004",
     "il 2 0 0",
-    "qq 2 0",
     "M2A104",
-    "il 2 0 1",
-    "M1C002",
-    "rq 2 0 0",
-    "M1C024",
-    "rq 2 0 1",
-    "il 1 2 0",
-    "M1C101",
-    "rq 1 1 1",
-    "M1C114",
-    "il 1 2 1",
-    "M3A102",
     "rq 1 1 0",
-    "M3A124",
-    "M3A004",
-    "M2B102",
-    "rq 1 2 1",
-    "out 0 1",
-    "M2B124",
-    "out 0 0",
+    "il 2 0 1",
+    "M1C001",
+    "rq 1 1 1",
+    "M1C014",
+    "il 1 2 0",
+    "M1C104",
+    "rq 2 0 1",
+    "il 1 2 1",
+    "M2B101",
+    "rq 2 0 0",
+    "M2B114",
     "il 2 1 1",
+    "M3A003",
     "rq 1 2 0",
+    "M3A034",
     "M2B004",
     "il 2 1 0",
-    "M2C002",
-    "rq 2 1 1",
-    "M2C024",
-    "il 2 2 0",
-    "rq 2 1 0",
+    "M3A101",
+    "rq 1 2 1",
+    "M3A114",
+    "out 0 0",
     "M2C104",
+    "rq 2 1 1",
+    "out 0 1",
     "il 2 2 1",
+    "rq 2 1 0",
+    "M2C004",
+    "il 2 2 0",
     "M3B104",
-    "rq 2 2 0",
     "rq 2 2 1",
-    "M3B004",
+    "M3B001",
+    "rq 2 2 0",
+    "M3B013",
     "out 1 1",
-    "M3C004",
-    "M3C101",
+    "M3B034",
+    "M3C104",
+    "M3C002",
     "out 1 0",
-    "M3C114",
-    "out 2 0",
+    "M3C024",
     "out 2 1",
+    "out 2 0",
 ]
 
 
@@ -129,8 +130,8 @@ def tile_dense_heat_steps_t1_kernel(tc, q, w, heater, inv_cap, out):
         def hbm_rows(x, c):
             return x[CH * c : CH * (c + 1), :].rearrange("(p b) k -> p b k", b=NB)
 
-        nc.gpsimd.dma_start(out=hv[:], in_=heater.rearrange("(g p t) -> p g t", g=2, t=4))
-        nc.gpsimd.dma_start(out=iv[:], in_=inv_cap.rearrange("(g p t) -> p g t", g=2, t=4))
+        make_identity(nc, ident[:])
+        nc.scalar.dma_start(out=hv[:], in_=heater.rearrange("(g p t) -> p g t", g=2, t=4))
         for x in LOADS:
             if x.startswith("w"):
                 h, g = int(x[1]), int(x[2])
@@ -141,7 +142,7 @@ def tile_dense_heat_steps_t1_kernel(tc, q, w, heater, inv_cap, out):
                 nc.sync.dma_start(out=qn[c][:, 2 * pr : 2 * pr + 2, :], in_=hbm_rows(q, c)[:, 2 * pr : 2 * pr + 2, :])
         nc.vector.memset(warm[:], 0.0)
         nc.scalar.copy(out=warm[:], in_=warm[:])
-        make_identity(nc, ident[:])
+        nc.gpsimd.dma_start(out=iv[:], in_=inv_cap.rearrange("(g p t) -> p g t", g=2, t=4))
 
         codes = {}
         wgrp = {}

@@ -13,98 +13,127 @@ U8 = mybir.dt.uint8
 FP8X4 = mybir.dt.float8_e4m3fn_x4
 ADD = mybir.AluOpType.add
 MULT = mybir.AluOpType.mult
+COPY = mybir.ActivationFunctionType.Copy
 
 P = 128
-CH = 512
-NCH = B // CH
-NB = CH // P
-LOADS = ['q0a','w00','q0b','w01','q1a','w10','w11','q1b','q2b','q2a']
-WENG = {"10":"SS","11":"VS","00":"VS","01":"VS"}
-TAILV = 2
+SIZES = [512, 512, 256, 256]
+NCH = len(SIZES)
+BASE = [sum(SIZES[:c]) for c in range(NCH)]
+LOADS = ['q0b', 'q0a', 'w00', 'w01', 'w11', 'q1a', 'w10', 'q1b', 'q2', 'q3']
+WENG = {'00': 'SV', '01': 'VS', '10': 'VS', '11': 'VS'}
+SCENG = {(0, 1): 'S', (2, 0): 'S', (3, 1): 'V', (3, 0): 'S', (1, 0): 'S', (2, 1): 'V', (0, 0): 'S'}
+ILENG = {(1, 3, 0): 'V'}
+OUTENG = {(2, 1): 'SSVV', (3, 0): 'SVVV', (2, 0): 'SSVS', (3, 1): 'SVSS', (1, 1): 'SSSS', (1, 0): 'SSSS'}
+FIRST = 0
 ORDER = [
-    "turn 0 0",
     "w 00 1",
     "turn 0 1",
+    "turn 0 0",
     "qq 0 0",
     "w 00 0",
-    "wq 00",
-    "w 01 1",
-    "turn 1 0",
     "w 01 0",
+    "w 01 1",
+    "wq 00",
     "qq 0 1",
-    "w 10 1",
-    "w 11 1",
-    "wq 01",
-    "qq 1 0",
-    "M1A002",
-    "w 10 0",
     "w 11 0",
-    "M1A023",
-    "wq 11",
+    "w 11 1",
+    "w 10 0",
+    "w 10 1",
+    "turn 1 0",
+    "wq 01",
     "wq 10",
-    "M1A034",
+    "M1A004",
     "turn 1 1",
+    "turn 2 0",
     "il 1 0 0",
-    "qq 1 1",
-    "turn 2 1",
+    "qq 1 0",
     "M1A104",
     "il 1 0 1",
+    "M1B102",
+    "qq 2 0",
+    "M1B124",
+    "rq 1 0 1",
+    "il 1 1 1",
     "M1B003",
-    "rq 1 0 0",
-    "turn 2 0",
-    "qq 2 1",
+    "turn 3 0",
     "M1B034",
     "il 1 1 0",
-    "M1B101",
-    "rq 1 0 1",
-    "M1B114",
-    "il 1 1 1",
-    "qq 2 0",
+    "rq 1 0 0",
+    "M1C004",
+    "il 1 2 0",
     "M2A004",
     "il 2 0 0",
+    "qq 3 0",
     "M2A104",
-    "rq 1 1 0",
     "il 2 0 1",
-    "M1C001",
-    "rq 1 1 1",
-    "M1C014",
-    "il 1 2 0",
+    "sc 0 0",
     "M1C104",
-    "rq 2 0 1",
     "il 1 2 1",
-    "M2B101",
+    "sc 0 1",
+    "M1D004",
+    "rq 1 1 1",
+    "il 1 3 0",
+    "M1D102",
+    "rq 1 1 0",
     "rq 2 0 0",
-    "M2B114",
+    "M1D124",
+    "il 1 3 1",
+    "M2B002",
+    "rq 2 0 1",
+    "M2B024",
+    "il 2 1 0",
+    "M2B104",
     "il 2 1 1",
-    "M3A003",
+    "M3A002",
+    "rq 1 2 1",
+    "M3A023",
     "rq 1 2 0",
     "M3A034",
-    "M2B004",
-    "il 2 1 0",
-    "M3A101",
-    "rq 1 2 1",
-    "M3A114",
-    "out 0 0",
-    "M2C104",
-    "rq 2 1 1",
-    "out 0 1",
-    "il 2 2 1",
     "rq 2 1 0",
-    "M2C004",
+    "M3A103",
+    "rq 2 1 1",
+    "M3A134",
+    "out 0 0",
+    "sc 1 1",
+    "M2C002",
+    "sc 1 0",
+    "M2C024",
     "il 2 2 0",
-    "M3B104",
-    "rq 2 2 1",
-    "M3B001",
+    "M3B101",
+    "rq 1 3 0",
+    "M3B112",
+    "rq 1 3 1",
+    "out 0 1",
+    "M3B124",
+    "sc 2 0",
+    "M2C104",
+    "il 2 2 1",
+    "M2D002",
     "rq 2 2 0",
+    "M2D024",
+    "il 2 3 0",
+    "M2D104",
+    "il 2 3 1",
+    "M3B001",
+    "rq 2 2 1",
+    "rq 2 3 0",
     "M3B013",
     "out 1 1",
+    "rq 2 3 1",
+    "sc 3 0",
     "M3B034",
-    "M3C104",
     "M3C002",
-    "out 1 0",
+    "sc 2 1",
     "M3C024",
-    "out 2 1",
+    "M3C104",
+    "sc 3 1",
+    "out 1 0",
+    "M3D004",
     "out 2 0",
+    "out 2 1",
+    "M3D104",
+    "out 3 0",
+    "out 3 1",
 ]
 
 
@@ -118,17 +147,24 @@ def tile_dense_heat_steps_t1_kernel(tc, q, w, heater, inv_cap, out):
 
         ident = keep.tile([P, P], F32, name="ident")
         warm = keep.tile([P, 1], F32, name="warm")
+        ivf = keep.tile([P, 2, 4], F32, name="ivf")
         hv = keep.tile([P, 2, 4], BF16, name="hv")
         iv = keep.tile([P, 2, 4], BF16, name="iv")
-        wraw = [keep.tile([P, 2, 4, 512], BF16, name="wraw%d" % h) for h in range(2)]
-        wcodes = keep.tile([P, 2, N], U32, name="wcodes", align_bytes=256)
-        wscales = keep.tile([P, 2, N], U8, name="wscales", align_bytes=256)
-        qn = [keep.tile([P, NB, N], BF16, name="qn%d" % c) for c in range(NCH)]
-        qint = [keep.tile([P, 2, CH, 4], BF16, name="qint%d" % c, align_bytes=256) for c in range(NCH)]
-        state = [[keep.tile([P, 4, CH], F32, name="state%d%d" % (c, g)) for g in range(2)] for c in range(NCH)]
+        wraw = []
+        for h in range(2):
+            big = stage.tile([P, 2, 4, 512], BF16, name="big", align_bytes=256, bufs=8)
+            wraw.append(big)
+        wcodes = keep.tile([P, 2, 2, 512], U32, name="wcodes", align_bytes=256)
+        wscales = keep.tile([P, 2, 2, 512], U8, name="wscales", align_bytes=256)
+        qn = []
+        for c in range(NCH):
+            big = stage.tile([P, SIZES[c] // P, N], BF16, name="big", align_bytes=256, bufs=8)
+            qn.append(big)
+        qint = [keep.tile([P, 2, SIZES[c], 4], BF16, name="qint%d" % c, align_bytes=256) for c in range(NCH)]
+        state = [[keep.tile([P, 4, SIZES[c]], F32, name="state%d%d" % (c, g)) for g in range(2)] for c in range(NCH)]
 
         def hbm_rows(x, c):
-            return x[CH * c : CH * (c + 1), :].rearrange("(p b) k -> p b k", b=NB)
+            return x[BASE[c] : BASE[c] + SIZES[c], :].rearrange("(p b) k -> p b k", b=SIZES[c] // P)
 
         make_identity(nc, ident[:])
         nc.scalar.dma_start(out=hv[:], in_=heater.rearrange("(g p t) -> p g t", g=2, t=4))
@@ -138,11 +174,12 @@ def tile_dense_heat_steps_t1_kernel(tc, q, w, heater, inv_cap, out):
                 src = w[512 * g : 512 * (g + 1), 512 * h : 512 * (h + 1)].rearrange("(p j) c -> p j c", j=4)
                 nc.sync.dma_start(out=wraw[h][:, g, :, :], in_=src)
             else:
-                c, pr = int(x[1]), "ab".index(x[2])
+                c, pr = int(x[1]), ("ab".index(x[2]) if len(x) > 2 else 0)
                 nc.sync.dma_start(out=qn[c][:, 2 * pr : 2 * pr + 2, :], in_=hbm_rows(q, c)[:, 2 * pr : 2 * pr + 2, :])
         nc.vector.memset(warm[:], 0.0)
-        nc.scalar.copy(out=warm[:], in_=warm[:])
+        nc.scalar.activation(warm[:], warm[:], COPY, scale=1.0)
         nc.gpsimd.dma_start(out=iv[:], in_=inv_cap.rearrange("(g p t) -> p g t", g=2, t=4))
+        nc.gpsimd.tensor_copy(out=ivf[:], in_=iv[:])
 
         codes = {}
         wgrp = {}
@@ -150,23 +187,29 @@ def tile_dense_heat_steps_t1_kernel(tc, q, w, heater, inv_cap, out):
 
         def get_codes(s, c):
             if (s, c) not in codes:
-                cd = keep.tile([P, 2, CH], U32, name="codes%d%d" % (s % 2, c), align_bytes=256)
-                sc = keep.tile([P, 2, CH], U8, name="scales%d%d" % (s % 2, c), align_bytes=256)
+                cd = keep.tile([P, 2, SIZES[c]], U32, name="codes%d%d" % (s % 2, c), align_bytes=256)
+                sc = keep.tile([P, 2, SIZES[c]], U8, name="scales%d%d" % (s % 2, c), align_bytes=256)
                 codes[(s, c)] = (cd, sc)
             return codes[(s, c)]
 
         def do_wq(h, g):
-            cols = slice(512 * h, 512 * (h + 1))
-            nc.vector.quantize_mx(out=wcodes[:, g, cols].bitcast(FP8X4), scales=wscales[:, g, cols], in_=wgrp[(h, g)][:])
+            if h == 0:
+                nc.vector.quantize_mx(out=wcodes[:, 0, g, :].bitcast(FP8X4), scales=wscales[:, 0, g, :], in_=wgrp[0][:, g, :])
+            else:
+                nc.vector.quantize_mx(
+                    out=wcodes[:, 1].rearrange("p g c -> p (g c)").bitcast(FP8X4),
+                    scales=wscales[:, 1].rearrange("p g c -> p (g c)"),
+                    in_=wgrp[1][:].rearrange("p g c -> p (g c)"),
+                )
 
         def do_w(h, g, hf):
-            if (h, g) not in wgrp:
-                new = stage.tile([P, 2048], BF16, name="wgrp", align_bytes=256, bufs=4)
-                wgrp[(h, g)] = new
+            if h not in wgrp:
+                big = stage.tile([P, 2, 2048], BF16, name="big", align_bytes=256, bufs=8)
+                wgrp[h] = big
             copy = nc.vector.tensor_copy if WENG["%d%d" % (h, g)][hf] == "V" else nc.scalar.copy
             ts = slice(2 * hf, 2 * hf + 2)
             copy(
-                out=wgrp[(h, g)][:].rearrange("p (t m j) -> p t m j", t=4, j=4)[:, ts],
+                out=wgrp[h][:, g, :].rearrange("p (t m j) -> p t m j", t=4, j=4)[:, ts],
                 in_=wraw[h][:, g, :, :].rearrange("p j (m t) -> p t m j", t=4)[:, ts],
             )
 
@@ -182,45 +225,77 @@ def tile_dense_heat_steps_t1_kernel(tc, q, w, heater, inv_cap, out):
 
         def do_qq(c, pr):
             cd, sc = get_codes(1, c)
+            if c:
+                nc.vector.quantize_mx(
+                    out=cd[:].rearrange("p g n -> p (g n)").bitcast(FP8X4),
+                    scales=sc[:].rearrange("p g n -> p (g n)"),
+                    in_=qint[c][:].rearrange("p g n t -> p (g n t)"),
+                )
+                return
             cols = slice(256 * pr, 256 * (pr + 1))
             for g in range(2):
                 nc.vector.quantize_mx(out=cd[:, g, cols].bitcast(FP8X4), scales=sc[:, g, cols], in_=qint[c][:, g, cols, :].rearrange("p n t -> p (n t)"))
 
-        def do_mx(s, c, go, t):
+        def one_pass(dst, s, c, go, t, g):
             cd, sc = get_codes(s, c)
-            bank = psum.tile([P, CH], F32, name="bank")
-            cols = slice(512 * go + 128 * t, 512 * go + 128 * (t + 1))
-            for g in range(2):
-                nc.tensor.matmul_mx(
-                    out=bank[:],
-                    lhsT=wcodes[:, g, cols].bitcast(FP8X4),
-                    lhsT_scale=wscales[:, g, cols],
-                    rhs=cd[:, g, :].bitcast(FP8X4),
-                    rhs_scale=sc[:, g, :],
-                    start=(g == 0),
-                    stop=(g == 1),
-                )
-            st = state[c][go][:, t, :]
-            if s == 1:
-                nc.vector.scalar_tensor_tensor(st, bank[:], hv[:, go, t : t + 1], qint[c][:, go, :, t], ADD, ADD)
-            elif s == 2:
-                nc.vector.scalar_tensor_tensor(st, bank[:], hv[:, go, t : t + 1], st, ADD, ADD)
+            cols = slice(128 * t, 128 * (t + 1))
+            nc.tensor.matmul_mx(
+                out=dst,
+                lhsT=wcodes[:, go, g, cols].bitcast(FP8X4),
+                lhsT_scale=wscales[:, go, g, cols],
+                rhs=cd[:, g, :].bitcast(FP8X4),
+                rhs_scale=sc[:, g, :],
+                start=(g == 0),
+                stop=(g == 1),
+            )
+
+        first_banks = []
+
+        def do_mx(s, c, go, t0):
+            n = SIZES[c]
+            per = 512 // n
+            if (s, c, go) == (1, 0, FIRST) and n == 512:
+                if t0 == 0:
+                    for tt in range(4):
+                        bank = psum.tile([P, 512], F32, name="bank")
+                        first_banks.append(bank)
+                        one_pass(bank[:], s, c, go, tt, 0)
+                bank = first_banks[t0]
+                one_pass(bank[:], s, c, go, t0, 1)
             else:
-                nc.vector.scalar_tensor_tensor(st, bank[:], iv[:, go, t : t + 1], st, MULT, ADD)
+                bank = psum.tile([P, 512], F32, name="bank")
+                for j in range(per):
+                    for g in range(2):
+                        one_pass(bank[:, n * j : n * (j + 1)], s, c, go, t0 + j, g)
+            for j in reversed(range(per)):
+                t = t0 + j
+                src = bank[:, n * j : n * (j + 1)]
+                st = state[c][go][:, t, :]
+                if s == 1:
+                    nc.vector.scalar_tensor_tensor(st, src, hv[:, go, t : t + 1], qint[c][:, go, :, t], ADD, ADD)
+                elif s == 2:
+                    nc.vector.scalar_tensor_tensor(st, src, hv[:, go, t : t + 1], st, ADD, ADD)
+                else:
+                    nc.vector.scalar_tensor_tensor(st, src, iv[:, go, t : t + 1], st, MULT, ADD)
 
         def do_il(s, c, go):
-            grouped = stage.tile([P, CH, 4], BF16, name="grp", align_bytes=256)
-            for n0 in (0, 256):
+            grouped = stage.tile([P, SIZES[c], 4], BF16, name="grp", align_bytes=256, bufs=8)
+            for n0 in range(0, SIZES[c], 256):
                 n = slice(n0, n0 + 256)
-                nc.scalar.copy(
+                copy = nc.vector.tensor_copy if ILENG.get((s, c, go)) == "V" else nc.scalar.copy
+                copy(
                     out=grouped[:, n, :].rearrange("p (c i) t -> p c t i", i=4),
                     in_=state[c][go][:, :, n].rearrange("p t (c i) -> p c t i", i=4),
                 )
             grp[(s, c, go)] = grouped
-            if s == 2:
-                for t in range(4):
-                    st = state[c][go][:, t, :]
-                    nc.gpsimd.tensor_scalar(st, st, iv[:, go, t : t + 1], 0.0, MULT, ADD)
+
+        def do_sc(c, go):
+            for t in range(4):
+                st = state[c][go][:, t, :]
+                if SCENG.get((c, go)) == "S":
+                    nc.scalar.activation(st, st, COPY, scale=ivf[:, go, t : t + 1])
+                else:
+                    nc.vector.tensor_scalar_mul(st, st, ivf[:, go, t : t + 1])
 
         def do_rq(s, c, go):
             cd, sc = get_codes(s + 1, c)
@@ -231,21 +306,34 @@ def tile_dense_heat_steps_t1_kernel(tc, q, w, heater, inv_cap, out):
         def do_out(c, go):
             count["out"] += 1
             dst = hbm_rows(out, c)
-            res = stage.tile([P, NB, 512], F32, name="res")
-            for b in range(NB):
-                bank = psum.tile([P, 4, P], F32, name="bank")
+            nb = SIZES[c] // P
+            res = stage.tile([P, nb, 512], F32, name="big", align_bytes=256, bufs=8)
+            last = count["out"] == 2 * NCH
+            banks = []
+            if last:
+                for b in range(nb):
+                    bank = psum.tile([P, 4, P], F32, name="bank")
+                    banks.append(bank)
                 for t in range(4):
-                    nc.tensor.transpose(bank[:, t, :], state[c][go][:, t, P * b : P * (b + 1)], ident[:])
-                copy = nc.vector.tensor_copy if count["out"] > 6 - TAILV and b % 2 == 1 else nc.scalar.copy
+                    for b in range(nb):
+                        nc.tensor.transpose(banks[b][:, t, :], state[c][go][:, t, P * b : P * (b + 1)], ident[:])
+            for b in range(nb):
+                if last:
+                    bank = banks[b]
+                else:
+                    bank = psum.tile([P, 4, P], F32, name="bank")
+                    for t in range(4):
+                        nc.tensor.transpose(bank[:, t, :], state[c][go][:, t, P * b : P * (b + 1)], ident[:])
+                copy = nc.vector.tensor_copy if OUTENG.get((c, go), "SVSV" if last else "SSSS")[b] == "V" else nc.scalar.copy
                 copy(out=res[:, b, :].rearrange("p (m t) -> p m t", t=4), in_=bank[:].rearrange("p t m -> p m t"))
                 nc.sync.dma_start(out=dst[:, b, 512 * go : 512 * (go + 1)], in_=res[:, b, :])
 
-        table = {"turn": do_turn, "qq": do_qq, "il": do_il, "rq": do_rq, "out": do_out}
+        table = {"turn": do_turn, "qq": do_qq, "il": do_il, "rq": do_rq, "out": do_out, "sc": do_sc}
         for line in ORDER:
             if line.startswith("M"):
-                s, c, go = int(line[1]), "ABC".index(line[2]), int(line[3])
+                s, c, go = int(line[1]), "ABCD".index(line[2]), int(line[3])
                 first = int(line[4])
-                for t in range(first, int(line[5])):
+                for t in range(first, int(line[5]), 512 // SIZES[c]):
                     do_mx(s, c, go, t)
             else:
                 parts = line.split(" ")

from contextlib import ExitStack

import concourse.mybir as mybir
from concourse.masks import make_identity

B, N = 1536, 1024
FLOPS = 3 * 2 * B * N * N

F32 = mybir.dt.float32
BF16 = mybir.dt.bfloat16
U32 = mybir.dt.uint32
U8 = mybir.dt.uint8
FP8X4 = mybir.dt.float8_e4m3fn_x4
ADD = mybir.AluOpType.add
MULT = mybir.AluOpType.mult
COPY = mybir.ActivationFunctionType.Copy

P = 128
SIZES = [512, 512, 256, 256]
NCH = len(SIZES)
BASE = [sum(SIZES[:c]) for c in range(NCH)]
LOADS = ['q0b', 'q0a', 'w00', 'w01', 'w11', 'q1a', 'w10', 'q1b', 'q2', 'q3']
WENG = {'00': 'SV', '01': 'VS', '10': 'VS', '11': 'VS'}
SCENG = {(0, 1): 'S', (2, 0): 'S', (3, 1): 'V', (3, 0): 'S', (1, 0): 'S', (2, 1): 'V', (0, 0): 'S'}
ILENG = {(1, 3, 0): 'V'}
OUTENG = {(2, 1): 'SSVV', (3, 0): 'SVVV', (2, 0): 'SSVS', (3, 1): 'SVSS', (1, 1): 'SSSS', (1, 0): 'SSSS'}
FIRST = 0
ORDER = [
    "w 00 1",
    "turn 0 1",
    "turn 0 0",
    "qq 0 0",
    "w 00 0",
    "w 01 0",
    "w 01 1",
    "wq 00",
    "qq 0 1",
    "w 11 0",
    "w 11 1",
    "w 10 0",
    "w 10 1",
    "turn 1 0",
    "wq 01",
    "wq 10",
    "M1A004",
    "turn 1 1",
    "turn 2 0",
    "il 1 0 0",
    "qq 1 0",
    "M1A104",
    "il 1 0 1",
    "M1B102",
    "qq 2 0",
    "M1B124",
    "rq 1 0 1",
    "il 1 1 1",
    "M1B003",
    "turn 3 0",
    "M1B034",
    "il 1 1 0",
    "rq 1 0 0",
    "M1C004",
    "il 1 2 0",
    "M2A004",
    "il 2 0 0",
    "qq 3 0",
    "M2A104",
    "il 2 0 1",
    "sc 0 0",
    "M1C104",
    "il 1 2 1",
    "sc 0 1",
    "M1D004",
    "rq 1 1 1",
    "il 1 3 0",
    "M1D102",
    "rq 1 1 0",
    "rq 2 0 0",
    "M1D124",
    "il 1 3 1",
    "M2B002",
    "rq 2 0 1",
    "M2B024",
    "il 2 1 0",
    "M2B104",
    "il 2 1 1",
    "M3A002",
    "rq 1 2 1",
    "M3A023",
    "rq 1 2 0",
    "M3A034",
    "rq 2 1 0",
    "M3A103",
    "rq 2 1 1",
    "M3A134",
    "out 0 0",
    "sc 1 1",
    "M2C002",
    "sc 1 0",
    "M2C024",
    "il 2 2 0",
    "M3B101",
    "rq 1 3 0",
    "M3B112",
    "rq 1 3 1",
    "out 0 1",
    "M3B124",
    "sc 2 0",
    "M2C104",
    "il 2 2 1",
    "M2D002",
    "rq 2 2 0",
    "M2D024",
    "il 2 3 0",
    "M2D104",
    "il 2 3 1",
    "M3B001",
    "rq 2 2 1",
    "rq 2 3 0",
    "M3B013",
    "out 1 1",
    "rq 2 3 1",
    "sc 3 0",
    "M3B034",
    "M3C002",
    "sc 2 1",
    "M3C024",
    "M3C104",
    "sc 3 1",
    "out 1 0",
    "M3D004",
    "out 2 0",
    "out 2 1",
    "M3D104",
    "out 3 0",
    "out 3 1",
]


def tile_dense_heat_steps_t1_kernel(tc, q, w, heater, inv_cap, out):
    nc = tc.nc
    with ExitStack() as ctx:
        keep = ctx.enter_context(tc.tile_pool(name="keep", bufs=1))
        stage = ctx.enter_context(tc.tile_pool(name="stage", bufs=3))
        psum = ctx.enter_context(tc.psum_pool(name="psum", bufs=8))
        ctx.enter_context(tc.manual_schedule())

        ident = keep.tile([P, P], F32, name="ident")
        warm = keep.tile([P, 1], F32, name="warm")
        ivf = keep.tile([P, 2, 4], F32, name="ivf")
        hv = keep.tile([P, 2, 4], BF16, name="hv")
        iv = keep.tile([P, 2, 4], BF16, name="iv")
        wraw = []
        for h in range(2):
            big = stage.tile([P, 2, 4, 512], BF16, name="big", align_bytes=256, bufs=8)
            wraw.append(big)
        wcodes = keep.tile([P, 2, 2, 512], U32, name="wcodes", align_bytes=256)
        wscales = keep.tile([P, 2, 2, 512], U8, name="wscales", align_bytes=256)
        qn = []
        for c in range(NCH):
            big = stage.tile([P, SIZES[c] // P, N], BF16, name="big", align_bytes=256, bufs=8)
            qn.append(big)
        qint = [keep.tile([P, 2, SIZES[c], 4], BF16, name="qint%d" % c, align_bytes=256) for c in range(NCH)]
        state = [[keep.tile([P, 4, SIZES[c]], F32, name="state%d%d" % (c, g)) for g in range(2)] for c in range(NCH)]

        def hbm_rows(x, c):
            return x[BASE[c] : BASE[c] + SIZES[c], :].rearrange("(p b) k -> p b k", b=SIZES[c] // P)

        make_identity(nc, ident[:])
        nc.scalar.dma_start(out=hv[:], in_=heater.rearrange("(g p t) -> p g t", g=2, t=4))
        for x in LOADS:
            if x.startswith("w"):
                h, g = int(x[1]), int(x[2])
                src = w[512 * g : 512 * (g + 1), 512 * h : 512 * (h + 1)].rearrange("(p j) c -> p j c", j=4)
                nc.sync.dma_start(out=wraw[h][:, g, :, :], in_=src)
            else:
                c, pr = int(x[1]), ("ab".index(x[2]) if len(x) > 2 else 0)
                nc.sync.dma_start(out=qn[c][:, 2 * pr : 2 * pr + 2, :], in_=hbm_rows(q, c)[:, 2 * pr : 2 * pr + 2, :])
        nc.vector.memset(warm[:], 0.0)
        nc.scalar.activation(warm[:], warm[:], COPY, scale=1.0)
        nc.gpsimd.dma_start(out=iv[:], in_=inv_cap.rearrange("(g p t) -> p g t", g=2, t=4))
        nc.gpsimd.tensor_copy(out=ivf[:], in_=iv[:])

        codes = {}
        wgrp = {}
        grp = {}

        def get_codes(s, c):
            if (s, c) not in codes:
                cd = keep.tile([P, 2, SIZES[c]], U32, name="codes%d%d" % (s % 2, c), align_bytes=256)
                sc = keep.tile([P, 2, SIZES[c]], U8, name="scales%d%d" % (s % 2, c), align_bytes=256)
                codes[(s, c)] = (cd, sc)
            return codes[(s, c)]

        def do_wq(h, g):
            if h == 0:
                nc.vector.quantize_mx(out=wcodes[:, 0, g, :].bitcast(FP8X4), scales=wscales[:, 0, g, :], in_=wgrp[0][:, g, :])
            else:
                nc.vector.quantize_mx(
                    out=wcodes[:, 1].rearrange("p g c -> p (g c)").bitcast(FP8X4),
                    scales=wscales[:, 1].rearrange("p g c -> p (g c)"),
                    in_=wgrp[1][:].rearrange("p g c -> p (g c)"),
                )

        def do_w(h, g, hf):
            if h not in wgrp:
                big = stage.tile([P, 2, 2048], BF16, name="big", align_bytes=256, bufs=8)
                wgrp[h] = big
            copy = nc.vector.tensor_copy if WENG["%d%d" % (h, g)][hf] == "V" else nc.scalar.copy
            ts = slice(2 * hf, 2 * hf + 2)
            copy(
                out=wgrp[h][:, g, :].rearrange("p (t m j) -> p t m j", t=4, j=4)[:, ts],
                in_=wraw[h][:, g, :, :].rearrange("p j (m t) -> p t m j", t=4)[:, ts],
            )

        def do_turn(c, pr):
            for b in (2 * pr, 2 * pr + 1):
                words = qn[c][:, b, :].bitcast(F32)
                bank = psum.tile([P, 4, P], F32, name="bank")
                for g in range(2):
                    for u in range(2):
                        nc.tensor.transpose(bank[:, 2 * g + u, :], words[:, 256 * g + u : 256 * (g + 1) : 2], ident[:])
                dst = qint[c][:, :, P * b : P * (b + 1), :].rearrange("p g n t -> p g (n t)").bitcast(F32)
                nc.scalar.copy(out=dst.rearrange("p g (n u) -> p g n u", u=2), in_=bank[:].rearrange("p (g u) n -> p g n u", g=2))

        def do_qq(c, pr):
            cd, sc = get_codes(1, c)
            if c:
                nc.vector.quantize_mx(
                    out=cd[:].rearrange("p g n -> p (g n)").bitcast(FP8X4),
                    scales=sc[:].rearrange("p g n -> p (g n)"),
                    in_=qint[c][:].rearrange("p g n t -> p (g n t)"),
                )
                return
            cols = slice(256 * pr, 256 * (pr + 1))
            for g in range(2):
                nc.vector.quantize_mx(out=cd[:, g, cols].bitcast(FP8X4), scales=sc[:, g, cols], in_=qint[c][:, g, cols, :].rearrange("p n t -> p (n t)"))

        def one_pass(dst, s, c, go, t, g):
            cd, sc = get_codes(s, c)
            cols = slice(128 * t, 128 * (t + 1))
            nc.tensor.matmul_mx(
                out=dst,
                lhsT=wcodes[:, go, g, cols].bitcast(FP8X4),
                lhsT_scale=wscales[:, go, g, cols],
                rhs=cd[:, g, :].bitcast(FP8X4),
                rhs_scale=sc[:, g, :],
                start=(g == 0),
                stop=(g == 1),
            )

        first_banks = []

        def do_mx(s, c, go, t0):
            n = SIZES[c]
            per = 512 // n
            if (s, c, go) == (1, 0, FIRST) and n == 512:
                if t0 == 0:
                    for tt in range(4):
                        bank = psum.tile([P, 512], F32, name="bank")
                        first_banks.append(bank)
                        one_pass(bank[:], s, c, go, tt, 0)
                bank = first_banks[t0]
                one_pass(bank[:], s, c, go, t0, 1)
            else:
                bank = psum.tile([P, 512], F32, name="bank")
                for j in range(per):
                    for g in range(2):
                        one_pass(bank[:, n * j : n * (j + 1)], s, c, go, t0 + j, g)
            for j in reversed(range(per)):
                t = t0 + j
                src = bank[:, n * j : n * (j + 1)]
                st = state[c][go][:, t, :]
                if s == 1:
                    nc.vector.scalar_tensor_tensor(st, src, hv[:, go, t : t + 1], qint[c][:, go, :, t], ADD, ADD)
                elif s == 2:
                    nc.vector.scalar_tensor_tensor(st, src, hv[:, go, t : t + 1], st, ADD, ADD)
                else:
                    nc.vector.scalar_tensor_tensor(st, src, iv[:, go, t : t + 1], st, MULT, ADD)

        def do_il(s, c, go):
            grouped = stage.tile([P, SIZES[c], 4], BF16, name="grp", align_bytes=256, bufs=8)
            for n0 in range(0, SIZES[c], 256):
                n = slice(n0, n0 + 256)
                copy = nc.vector.tensor_copy if ILENG.get((s, c, go)) == "V" else nc.scalar.copy
                copy(
                    out=grouped[:, n, :].rearrange("p (c i) t -> p c t i", i=4),
                    in_=state[c][go][:, :, n].rearrange("p t (c i) -> p c t i", i=4),
                )
            grp[(s, c, go)] = grouped

        def do_sc(c, go):
            for t in range(4):
                st = state[c][go][:, t, :]
                if SCENG.get((c, go)) == "S":
                    nc.scalar.activation(st, st, COPY, scale=ivf[:, go, t : t + 1])
                else:
                    nc.vector.tensor_scalar_mul(st, st, ivf[:, go, t : t + 1])

        def do_rq(s, c, go):
            cd, sc = get_codes(s + 1, c)
            nc.vector.quantize_mx(out=cd[:, go, :].bitcast(FP8X4), scales=sc[:, go, :], in_=grp[(s, c, go)][:].rearrange("p n t -> p (n t)"))

        count = {"out": 0}

        def do_out(c, go):
            count["out"] += 1
            dst = hbm_rows(out, c)
            nb = SIZES[c] // P
            res = stage.tile([P, nb, 512], F32, name="big", align_bytes=256, bufs=8)
            last = count["out"] == 2 * NCH
            banks = []
            if last:
                for b in range(nb):
                    bank = psum.tile([P, 4, P], F32, name="bank")
                    banks.append(bank)
                for t in range(4):
                    for b in range(nb):
                        nc.tensor.transpose(banks[b][:, t, :], state[c][go][:, t, P * b : P * (b + 1)], ident[:])
            for b in range(nb):
                if last:
                    bank = banks[b]
                else:
                    bank = psum.tile([P, 4, P], F32, name="bank")
                    for t in range(4):
                        nc.tensor.transpose(bank[:, t, :], state[c][go][:, t, P * b : P * (b + 1)], ident[:])
                copy = nc.vector.tensor_copy if OUTENG.get((c, go), "SVSV" if last else "SSSS")[b] == "V" else nc.scalar.copy
                copy(out=res[:, b, :].rearrange("p (m t) -> p m t", t=4), in_=bank[:].rearrange("p t m -> p m t"))
                nc.sync.dma_start(out=dst[:, b, 512 * go : 512 * (go + 1)], in_=res[:, b, :])

        table = {"turn": do_turn, "qq": do_qq, "il": do_il, "rq": do_rq, "out": do_out, "sc": do_sc}
        for line in ORDER:
            if line.startswith("M"):
                s, c, go = int(line[1]), "ABCD".index(line[2]), int(line[3])
                first = int(line[4])
                for t in range(first, int(line[5]), 512 // SIZES[c]):
                    do_mx(s, c, go, t)
            else:
                parts = line.split(" ")
                if parts[0] == "w":
                    do_w(int(parts[1][0]), int(parts[1][1]), int(parts[2]))
                elif parts[0] == "wq":
                    do_wq(int(parts[1][0]), int(parts[1][1]))
                else:
                    table[parts[0]](*[int(v) for v in parts[1:]])
